import numpy as np
import ml_dtypes


def mxq(x, axis, fmt="e4m3"):
    dtype, down = {"e4m3": (ml_dtypes.float8_e4m3fn, 7), "e5m2": (ml_dtypes.float8_e5m2, 14)}[fmt]
    v = np.moveaxis(np.asarray(x, np.float32).astype(ml_dtypes.bfloat16).astype(np.float64), axis, -1)
    blocks = v.reshape(v.shape[:-1] + (-1, 32))
    amax = np.abs(blocks).max(-1, keepdims=True)
    byte = np.maximum(np.where(amax > 0, np.frexp(amax)[1] - 1 + 127, 0) - down, 1)
    scale = np.exp2(byte - 127.0)
    codes = (blocks / scale).astype(np.float32).astype(dtype).astype(np.float64)
    return np.moveaxis((codes * scale).reshape(v.shape), -1, axis)


WIDE = False


def mx_kscale(k):
    if not WIDE:
        return np.ones(k)
    levels = np.array([10, -10, 5, -5, 0])
    if k % 512:
        return np.exp2(np.random.permutation(np.resize(levels, k // 32))).repeat(32)
    a = np.empty((k // 512, 16))
    for p in range(k // 512):
        a[p, :8] = np.random.permutation(np.resize(levels, 8))
        for g in range(8):
            far = levels[np.abs(levels - a[p, g]) >= 10]
            a[p, g + 8] = far[np.random.randint(len(far))]
    return np.exp2(a.ravel()).repeat(32)


def f64(x):
    return np.asarray(x).astype(np.float64)


def striped(idx):
    return np.tile(np.asarray(idx).reshape(-1, 16).T, (8, 1)).astype(np.uint16)


def unstriped(offs):
    return offs[:16].T.reshape(-1).astype(np.int64)


E2M1 = np.array([0.0, 0.5, 1.0, 1.5, 2.0, 3.0, 4.0, 6.0, -0.0, -0.5, -1.0, -1.5, -2.0, -3.0, -4.0, -6.0])


def pack_weight(w, fmt):
    k, n = w.shape
    w = f64(np.asarray(w, np.float32).astype(ml_dtypes.bfloat16)).reshape(k // 32, 32, n)
    amax = np.abs(w).max(1)
    if fmt == "e4m3":
        byte = np.frexp(amax)[1] - 1 + 127 - 7
    else:
        mant, ex = np.frexp(amax / 6.0)
        byte = np.where(mant > 0.5, ex, ex - 1) + 127
    byte = np.clip(np.where(amax > 0, byte, 1), 1, 254)
    scaled = (w * np.exp2(127.0 - byte)[:, None, :]).reshape(k, n).astype(np.float32)
    by_word = np.ascontiguousarray(scaled.reshape(k // 512, 128, 4, n).transpose(0, 1, 3, 2))
    if fmt == "e4m3":
        words = by_word.astype(ml_dtypes.float8_e4m3fn).view(np.uint8)
    else:
        c = by_word.astype(ml_dtypes.float4_e2m1fn).view(np.uint8) & 0xF
        words = (c[..., 0::2] | (c[..., 1::2] << 4)).reshape(k // 512, 128, 2 * n)
    return np.ascontiguousarray(words), np.ascontiguousarray(byte.astype(np.uint8).reshape(k // 512, 16, n))


def unpack_weight(words, scales, fmt):
    g, _, n = scales.shape
    words = np.ascontiguousarray(words).reshape(g, 128, n, -1)
    if fmt == "e4m3":
        vals = words.view(ml_dtypes.float8_e4m3fn).astype(np.float64)
    else:
        nib = np.empty((g, 128, n, 4), np.uint8)
        nib[..., 0::2] = words & 0xF
        nib[..., 1::2] = words >> 4
        vals = E2M1[nib]
    vals = vals * np.repeat(np.exp2(scales.astype(np.float64) - 127.0), 8, axis=1)[..., None]
    return vals.transpose(0, 1, 3, 2).reshape(g * 512, n)


def sgn(shape):
    return np.random.uniform(0.5, 2.0, shape) * np.where(np.random.standard_normal(shape) < 0, -1.0, 1.0)


K, T, J, R, V, O, N = 512, 1024, 256, 512, 1024, 128, 256


def setup_inputs():
    n = np.random.standard_normal
    idx = np.random.permutation(V)[:R]
    idx2 = np.random.permutation(T)[:J]
    idx3 = np.random.permutation(J)[:O]
    fk = mx_kscale(K)
    fr = mx_kscale(R)
    xtp = pack_weight(n((K, T)) / fk[:, None], "e4m3")
    wtp = pack_weight(n((K, V)) * 1 / np.sqrt(K) * fk[:, None], "e2m1")
    wbp = pack_weight(n((R, N)) * 1 / np.sqrt(R) / fr[:, None], "e2m1")
    wcp = pack_weight(n((R, N)) * 1 / np.sqrt(R) / fr[:, None], "e4m3")
    return {
        "xt_words": xtp[0],
        "xt_scales": xtp[1],
        "wt_words": wtp[0],
        "wt_scales": wtp[1],
        "sa": (0.25 * sgn((R, 1))).astype(np.float32),
        "lf": (np.random.uniform(-0.4, 0.4, (R, 1)) + np.log(fr)[:, None]).astype(np.float32),
        "sb": (0.25 * sgn((R, 1))).astype(np.float32),
        "ls": (np.random.uniform(-0.4, 0.4, (R, 1)) + np.log(fr)[:, None]).astype(np.float32),
        "wb_words": wbp[0],
        "wb_scales": wbp[1],
        "wc_words": wcp[0],
        "wc_scales": wcp[1],
        "offs": striped(idx),
        "offs2": striped(idx2),
        "offs3": striped(idx3),
    }


def reference(xt_words, xt_scales, wt_words, wt_scales, sa, lf, sb, ls, wb_words, wb_scales, wc_words, wc_scales, offs, offs2, offs3):
    idx = unstriped(offs)
    idx2 = unstriped(offs2)
    idx3 = unstriped(offs3)
    xtu = unpack_weight(xt_words, xt_scales, "e4m3")
    wtu = unpack_weight(wt_words, wt_scales, "e2m1")
    wbu = unpack_weight(wb_words, wb_scales, "e2m1")
    wcu = unpack_weight(wc_words, wc_scales, "e4m3")
    wtidxg = wtu[:, idx]
    xtidx2g = xtu[:, idx2]
    a = wtidxg.T @ xtidx2g
    z1 = np.exp(a[:, idx3] * f64(sa) + f64(lf))
    z2 = np.exp(a[:, idx3] * f64(sb) + f64(ls))
    z1q = mxq(z1, 0, "e4m3")
    p = wbu.T @ z1q
    z2q = mxq(z2, 0, "e4m3")
    d = wcu.T @ z2q
    y = np.maximum(p, d)
    return y

from contextlib import ExitStack

import concourse.mybir as mybir

K, T, J, R, V, O, N = 512, 1024, 256, 512, 1024, 128, 256
FLOPS = 2 * K * R * J + 2 * 2 * R * N * O

F32 = mybir.dt.float32
BF16 = mybir.dt.bfloat16
I32 = mybir.dt.int32
U32 = mybir.dt.uint32
U16 = mybir.dt.uint16
U8 = mybir.dt.uint8
FP8X4 = mybir.dt.float8_e4m3fn_x4
FP4X4 = mybir.dt.float4_e2m1fn_x4
EXP = mybir.ActivationFunctionType.Exp
MAX = mybir.AluOpType.max

P = 128
PACK = 4
QUADS = 4
ALIGN = 64


def load_scale_rows(queue, plane, scales):
    for q in range(QUADS):
        queue.dma_start(plane[32 * q : 32 * q + 4, :].bitcast(I32), scales[0, 4 * q : 4 * q + 4, :].bitcast(I32))


def tile_list_twoheats_kernel(
    tc, xt_words, xt_scales, wt_words, wt_scales, sa, lf, sb, ls,
    wb_words, wb_scales, wc_words, wc_scales, offs, offs2, offs3, out,
):
    nc = tc.nc
    with ExitStack() as ctx:
        pool = ctx.enter_context(tc.tile_pool(name="held", bufs=1))
        psum = ctx.enter_context(tc.psum_pool(name="psum", bufs=1))

        def held(name, shape, dtype):
            return pool.tile(shape, dtype, name=name, align_bytes=ALIGN)

        feature_list = pool.tile([P, R // 16], U16, name="feature_list")
        token_list = pool.tile([P, J // 16], U16, name="token_list")
        slot_list = pool.tile([P, O // 16], U16, name="slot_list")

        wt_table = held("wt_table", [P, V], U16)
        wt_plane = held("wt_plane", [P, V], U8)
        xt_table = held("xt_table", [P, T], U32)
        xt_plane = held("xt_plane", [P, T], U8)
        wb_codes = held("wb_codes", [P, N], U16)
        wb_plane = held("wb_plane", [P, N], U8)
        wc_codes = held("wc_codes", [P, N], U32)
        wc_plane = held("wc_plane", [P, N], U8)
        slope1 = held("slope1", [P, PACK], F32)
        level1 = held("level1", [P, PACK], F32)
        slope2 = held("slope2", [P, PACK], F32)
        level2 = held("level2", [P, PACK], F32)

        for plane in (wt_plane, xt_plane, wb_plane, wc_plane):
            nc.vector.memset(plane[:].bitcast(I32), 0)

        def load_column(queue, tile, vector):
            queue.dma_start(tile[:], vector.rearrange("(p t) o -> p (t o)", t=PACK))

        nc.sync.dma_start(feature_list[:], offs)
        nc.sync.dma_start(wt_table[:].bitcast(I32), wt_words[0].bitcast(I32))
        load_scale_rows(nc.scalar, wt_plane, wt_scales)
        nc.sync.dma_start(token_list[:], offs2)
        nc.sync.dma_start(xt_table[:].bitcast(I32), xt_words[0].rearrange("p n t -> p (n t)").bitcast(I32))
        load_scale_rows(nc.sync, xt_plane, xt_scales)
        nc.sync.dma_start(slot_list[:], offs3)
        load_column(nc.gpsimd, slope1, sa)
        load_column(nc.gpsimd, level1, lf)
        load_column(nc.sync, slope2, sb)
        load_column(nc.sync, level2, ls)
        nc.sync.dma_start(wb_codes[:].bitcast(I32), wb_words[0].bitcast(I32))
        load_scale_rows(nc.sync, wb_plane, wb_scales)
        nc.sync.dma_start(wc_codes[:].bitcast(I32), wc_words[0].rearrange("p n t -> p (n t)").bitcast(I32))
        load_scale_rows(nc.sync, wc_plane, wc_scales)

        w_listed = held("w_listed", [P, R], U16)
        w_scale = held("w_scale", [P, R], U8)
        x_codes = held("x_codes", [P, J], U32)
        x_scale = held("x_scale", [P, J], U8)
        nc.vector.tensor_copy(w_listed[:], wt_table[:].indirect(feature_list[:]))
        nc.vector.tensor_copy(
            w_scale[:].rearrange("p (t q) -> p q t", t=PACK), wt_plane[:].indirect(feature_list[:])
        )
        nc.vector.tensor_copy(x_codes[:], xt_table[:].indirect(token_list[:]))
        nc.vector.tensor_copy(x_scale[:], xt_plane[:].indirect(token_list[:]))

        a_rows = []
        for t in range(PACK):
            w_codes = held("w_codes%d" % t, [P, P], U16)
            nc.vector.tensor_copy(w_codes[:], w_listed[:, t:R:PACK])
            a_sum = psum.tile([P, J], F32, name="a_sum%d" % t)
            nc.tensor.matmul_mx(
                out=a_sum[:],
                lhsT=w_codes[:].bitcast(FP4X4),
                lhsT_scale=w_scale[:, t * P : (t + 1) * P],
                rhs=x_codes[:].bitcast(FP8X4),
                rhs_scale=x_scale[:],
                start=True,
                stop=True,
            )
            rows = held("a_rows%d" % t, [P, J], F32)
            nc.vector.tensor_copy(rows[:], a_sum[:])
            a_rows.append(rows)

        def heat(name, slope, level, order):
            z = held(name, [P, PACK * O], BF16)
            for t in order:
                nc.scalar.activation(
                    z[:, t : PACK * O : PACK],
                    a_rows[t][:].indirect(slot_list[:]),
                    EXP,
                    bias=level[:, t : t + 1],
                    scale=slope[:, t : t + 1],
                )
            codes = held(name + "_codes", [P, O], U32)
            plane = held(name + "_plane", [P, O], U8)
            nc.vector.quantize_mx(out=codes[:].bitcast(FP8X4), scales=plane[:], in_=z[:])
            return codes, plane

        z1_codes, z1_plane = heat("z1", slope1, level1, range(PACK))
        p_sum = psum.tile([P, N], F32, name="p_sum")
        for h in range(N // P):
            cols = slice(h * P, (h + 1) * P)
            nc.tensor.matmul_mx(
                out=p_sum[:, cols],
                lhsT=wb_codes[:, cols].bitcast(FP4X4),
                lhsT_scale=wb_plane[:, cols],
                rhs=z1_codes[:].bitcast(FP8X4),
                rhs_scale=z1_plane[:],
                start=True,
                stop=True,
            )
        p_rows = held("p_rows", [P, N], F32)
        nc.vector.tensor_copy(p_rows[:], p_sum[:])

        z2_codes, z2_plane = heat("z2", slope2, level2, reversed(range(PACK)))
        for h, queue in enumerate((nc.sync, nc.scalar)):
            cols = slice(h * P, (h + 1) * P)
            d_sum = psum.tile([P, O], F32, name="d_sum%d" % h)
            nc.tensor.matmul_mx(
                out=d_sum[:],
                lhsT=wc_codes[:, cols].bitcast(FP8X4),
                lhsT_scale=wc_plane[:, cols],
                rhs=z2_codes[:].bitcast(FP8X4),
                rhs_scale=z2_plane[:],
                start=True,
                stop=True,
            )
            result = held("result%d" % h, [P, O], F32)
            nc.vector.tensor_tensor(result[:], d_sum[:], p_rows[:, cols], MAX)
            queue.dma_start(out[cols, :], result[:])
